import numpy as np
import ml_dtypes

BF16 = ml_dtypes.bfloat16


def bf(x):
    return np.asarray(x, np.float32).astype(BF16)


def f32(x):
    return np.asarray(x, np.float32)


def f64(x):
    return np.asarray(x).astype(np.float64)


def striped(idx):
    return np.tile(idx.reshape(-1, 16).T, (8, 1))


S, K, M, N, B, Q = 512, 128, 128, 192, 2, 96


def setup_inputs():
    return {"base": bf(np.random.standard_normal((B, M, S))), "x": bf(np.random.standard_normal((K, N))), "w": bf(np.random.standard_normal((K, M)) / np.sqrt(K)), "b": f32(0.5 * np.random.standard_normal((M, 1))), "offs": striped(np.random.permutation(S)[:N])}


def reference(base, x, w, b, offs):
    idx = offs[:16].T.reshape(-1)
    z = f64(base).copy()
    for i in range(B):
        z[i][:, idx[i * Q : (i + 1) * Q]] += f64(w).T @ f64(x)[:, i * Q : (i + 1) * Q]
    return z + f64(b)

@@ -1,0 +1,58 @@
+import concourse.mybir as mybir
+from concourse.masks import make_identity
+
+P = 128
+SEQS = 2
+TOKENS = 512
+PIECE = 96
+ENTRIES = SEQS * PIECE
+PIECE_COLS = PIECE // 16
+
+FLOPS = 2 * P * P * ENTRIES
+
+BF16 = mybir.dt.bfloat16
+F32 = mybir.dt.float32
+U16 = mybir.dt.uint16
+
+
+def tile_scatter_matmul_kernel(tc, base, x, w, b, offs, out):
+    nc = tc.nc
+    with (
+        tc.tile_pool(name="held", bufs=1) as held,
+        tc.psum_pool(name="windows", bufs=1) as windows,
+    ):
+        offsets = held.tile([P, ENTRIES // 16], U16, name="offsets")
+        nc.sync.dma_start(offsets[:], offs)
+        base_tiles = [held.tile([P, TOKENS], BF16, name=f"base{i}") for i in range(SEQS)]
+        nc.sync.dma_start(base_tiles[0][:], base[0])
+        nc.scalar.dma_start(base_tiles[1][:], base[1])
+        weights = held.tile([P, P], BF16, name="weights")
+        nc.scalar.dma_start(weights[:], w)
+        moving = held.tile([P, ENTRIES], BF16, name="moving")
+        nc.sync.dma_start(moving[:], x)
+        bias = held.tile([P, 1], F32, name="bias")
+        nc.scalar.dma_start(bias[:], b)
+
+        identity = held.tile([P, P], BF16, name="identity")
+        make_identity(nc, identity[:])
+
+        window_tiles = [windows.tile([P, TOKENS], F32, name=f"window{i}") for i in range(SEQS)]
+        for i in range(SEQS):
+            nc.tensor.matmul(window_tiles[i][:], identity[:], base_tiles[i][:], start=True, stop=False)
+
+        for i in range(SEQS):
+            nc.tensor.matmul(
+                window_tiles[i][:].indirect(offsets[:, i * PIECE_COLS : (i + 1) * PIECE_COLS]),
+                weights[:],
+                moving[:, i * PIECE : (i + 1) * PIECE],
+                start=False,
+                stop=True,
+            )
+
+        result_tiles = [held.tile([P, TOKENS], F32, name=f"result{i}") for i in range(SEQS)]
+        nc.vector.tensor_scalar_add(result_tiles[0][:], window_tiles[0][:], bias[:, 0:1])
+        nc.scalar.activation(
+            result_tiles[1][:], window_tiles[1][:], mybir.ActivationFunctionType.Identity, bias=bias[:, 0:1]
+        )
+        nc.sync.dma_start(out[0], result_tiles[0][:])
+        nc.scalar.dma_start(out[1], result_tiles[1][:])

@@ -8,6 +8,8 @@ PIECE = 96
 ENTRIES = SEQS * PIECE
 PIECE_COLS = PIECE // 16
 
+HALF = TOKENS // 2
+
 FLOPS = 2 * P * P * ENTRIES
 
 BF16 = mybir.dt.bfloat16
@@ -17,15 +19,16 @@ U16 = mybir.dt.uint16
 
 def tile_scatter_matmul_kernel(tc, base, x, w, b, offs, out):
     nc = tc.nc
+    identity_function = mybir.ActivationFunctionType.Identity
     with (
         tc.tile_pool(name="held", bufs=1) as held,
         tc.psum_pool(name="windows", bufs=1) as windows,
     ):
-        offsets = held.tile([P, ENTRIES // 16], U16, name="offsets")
-        nc.sync.dma_start(offsets[:], offs)
         base_tiles = [held.tile([P, TOKENS], BF16, name=f"base{i}") for i in range(SEQS)]
         nc.sync.dma_start(base_tiles[0][:], base[0])
         nc.scalar.dma_start(base_tiles[1][:], base[1])
+        offsets = held.tile([P, ENTRIES // 16], U16, name="offsets")
+        nc.sync.dma_start(offsets[:], offs)
         weights = held.tile([P, P], BF16, name="weights")
         nc.scalar.dma_start(weights[:], w)
         moving = held.tile([P, ENTRIES], BF16, name="moving")
@@ -35,6 +38,10 @@ def tile_scatter_matmul_kernel(tc, base, x, w, b, offs, out):
 
         identity = held.tile([P, P], BF16, name="identity")
         make_identity(nc, identity[:])
+
+        table_warmer = held.tile([P, 1], F32, name="table_warmer")
+        nc.vector.memset(table_warmer[:], 0.0)
+        nc.scalar.activation(table_warmer[:], table_warmer[:], identity_function)
 
         window_tiles = [windows.tile([P, TOKENS], F32, name=f"window{i}") for i in range(SEQS)]
         for i in range(SEQS):
@@ -50,9 +57,12 @@ def tile_scatter_matmul_kernel(tc, base, x, w, b, offs, out):
             )
 
         result_tiles = [held.tile([P, TOKENS], F32, name=f"result{i}") for i in range(SEQS)]
-        nc.vector.tensor_scalar_add(result_tiles[0][:], window_tiles[0][:], bias[:, 0:1])
-        nc.scalar.activation(
-            result_tiles[1][:], window_tiles[1][:], mybir.ActivationFunctionType.Identity, bias=bias[:, 0:1]
-        )
-        nc.sync.dma_start(out[0], result_tiles[0][:])
-        nc.scalar.dma_start(out[1], result_tiles[1][:])
+        for h in range(2):
+            half = slice(h * HALF, (h + 1) * HALF)
+            nc.vector.tensor_scalar_add(result_tiles[0][:, half], window_tiles[0][:, half], bias[:, 0:1])
+            nc.sync.dma_start(out[0][:, half], result_tiles[0][:, half])
+            nc.scalar.activation(
+                result_tiles[1][:, half], window_tiles[1][:, half], identity_function, bias=bias[:, 0:1]
+            )
+            last_queue = nc.scalar if h == 1 else nc.sync
+            last_queue.dma_start(out[1][:, half], result_tiles[1][:, half])

@@ -9,6 +9,7 @@ ENTRIES = SEQS * PIECE
 PIECE_COLS = PIECE // 16
 
 HALF = TOKENS // 2
+WARMERS = 12
 
 FLOPS = 2 * P * P * ENTRIES
 
@@ -35,6 +36,12 @@ def tile_scatter_matmul_kernel(tc, base, x, w, b, offs, out):
         nc.sync.dma_start(moving[:], x)
         bias = held.tile([P, 1], F32, name="bias")
         nc.scalar.dma_start(bias[:], b)
+
+        zeros = held.tile([P, P], BF16, name="zeros")
+        nc.vector.memset(zeros[:], 0.0)
+        unread = windows.tile([P, P], F32, name="unread")
+        for warmer in range(WARMERS):
+            nc.tensor.matmul(unread[:], zeros[:], zeros[:], start=True, stop=True)
 
         identity = held.tile([P, P], BF16, name="identity")
         make_identity(nc, identity[:])

@@ -25,9 +25,8 @@ def tile_scatter_matmul_kernel(tc, base, x, w, b, offs, out):
         tc.tile_pool(name="held", bufs=1) as held,
         tc.psum_pool(name="windows", bufs=1) as windows,
     ):
-        base_tiles = [held.tile([P, TOKENS], BF16, name=f"base{i}") for i in range(SEQS)]
-        nc.sync.dma_start(base_tiles[0][:], base[0])
-        nc.scalar.dma_start(base_tiles[1][:], base[1])
+        both_bases = held.tile([P, SEQS, TOKENS], BF16, name="both_bases")
+        nc.sync.dma_start(both_bases[:], base.rearrange("i m t -> m i t"))
         offsets = held.tile([P, ENTRIES // 16], U16, name="offsets")
         nc.sync.dma_start(offsets[:], offs)
         weights = held.tile([P, P], BF16, name="weights")
@@ -52,7 +51,7 @@ def tile_scatter_matmul_kernel(tc, base, x, w, b, offs, out):
 
         window_tiles = [windows.tile([P, TOKENS], F32, name=f"window{i}") for i in range(SEQS)]
         for i in range(SEQS):
-            nc.tensor.matmul(window_tiles[i][:], identity[:], base_tiles[i][:], start=True, stop=False)
+            nc.tensor.matmul(window_tiles[i][:], identity[:], both_bases[:, i, :], start=True, stop=False)
 
         for i in range(SEQS):
             nc.tensor.matmul(

@@ -8,7 +8,6 @@ PIECE = 96
 ENTRIES = SEQS * PIECE
 PIECE_COLS = PIECE // 16
 
-HALF = TOKENS // 2
 WARMERS = 12
 
 FLOPS = 2 * P * P * ENTRIES
@@ -63,12 +62,7 @@ def tile_scatter_matmul_kernel(tc, base, x, w, b, offs, out):
             )
 
         result_tiles = [held.tile([P, TOKENS], F32, name=f"result{i}") for i in range(SEQS)]
-        for h in range(2):
-            half = slice(h * HALF, (h + 1) * HALF)
-            nc.vector.tensor_scalar_add(result_tiles[0][:, half], window_tiles[0][:, half], bias[:, 0:1])
-            nc.sync.dma_start(out[0][:, half], result_tiles[0][:, half])
-            nc.scalar.activation(
-                result_tiles[1][:, half], window_tiles[1][:, half], identity_function, bias=bias[:, 0:1]
-            )
-            last_queue = nc.scalar if h == 1 else nc.sync
-            last_queue.dma_start(out[1][:, half], result_tiles[1][:, half])
+        nc.vector.tensor_scalar_add(result_tiles[0][:], window_tiles[0][:], bias[:, 0:1])
+        nc.sync.dma_start(out[0], result_tiles[0][:])
+        nc.scalar.activation(result_tiles[1][:], window_tiles[1][:], identity_function, bias=bias[:, 0:1])
+        nc.scalar.dma_start(out[1], result_tiles[1][:])

@@ -26,14 +26,14 @@ def tile_scatter_matmul_kernel(tc, base, x, w, b, offs, out):
     ):
         both_bases = held.tile([P, SEQS, TOKENS], BF16, name="both_bases")
         nc.sync.dma_start(both_bases[:], base.rearrange("i m t -> m i t"))
-        offsets = held.tile([P, ENTRIES // 16], U16, name="offsets")
-        nc.sync.dma_start(offsets[:], offs)
         weights = held.tile([P, P], BF16, name="weights")
-        nc.scalar.dma_start(weights[:], w)
+        nc.sync.dma_start(weights[:], w)
         moving = held.tile([P, ENTRIES], BF16, name="moving")
         nc.sync.dma_start(moving[:], x)
+        offsets = held.tile([P, ENTRIES // 16], U16, name="offsets")
+        nc.sync.dma_start(offsets[:], offs)
         bias = held.tile([P, 1], F32, name="bias")
-        nc.scalar.dma_start(bias[:], b)
+        nc.sync.dma_start(bias[:], b)
 
         zeros = held.tile([P, P], BF16, name="zeros")
         nc.vector.memset(zeros[:], 0.0)

@@ -8,7 +8,8 @@ PIECE = 96
 ENTRIES = SEQS * PIECE
 PIECE_COLS = PIECE // 16
 
-WARMERS = 12
+CLOCK_BAR_COLUMNS = 1024
+WARMERS = CLOCK_BAR_COLUMNS // P
 
 FLOPS = 2 * P * P * ENTRIES
 

@@ -63,7 +63,7 @@ def tile_scatter_matmul_kernel(tc, base, x, w, b, offs, out):
             )
 
         result_tiles = [held.tile([P, TOKENS], F32, name=f"result{i}") for i in range(SEQS)]
-        nc.vector.tensor_scalar_add(result_tiles[0][:], window_tiles[0][:], bias[:, 0:1])
-        nc.sync.dma_start(out[0], result_tiles[0][:])
-        nc.scalar.activation(result_tiles[1][:], window_tiles[1][:], identity_function, bias=bias[:, 0:1])
-        nc.scalar.dma_start(out[1], result_tiles[1][:])
+        nc.scalar.activation(result_tiles[0][:], window_tiles[0][:], identity_function, bias=bias[:, 0:1])
+        nc.scalar.dma_start(out[0], result_tiles[0][:])
+        nc.vector.tensor_scalar_add(result_tiles[1][:], window_tiles[1][:], bias[:, 0:1])
+        nc.sync.dma_start(out[1], result_tiles[1][:])

@@ -66,4 +66,4 @@ def tile_scatter_matmul_kernel(tc, base, x, w, b, offs, out):
         nc.scalar.activation(result_tiles[0][:], window_tiles[0][:], identity_function, bias=bias[:, 0:1])
         nc.scalar.dma_start(out[0], result_tiles[0][:])
         nc.vector.tensor_scalar_add(result_tiles[1][:], window_tiles[1][:], bias[:, 0:1])
-        nc.sync.dma_start(out[1], result_tiles[1][:])
+        nc.scalar.dma_start(out[1], result_tiles[1][:])

import concourse.mybir as mybir
from concourse.masks import make_identity

P = 128
SEQS = 2
TOKENS = 512
PIECE = 96
ENTRIES = SEQS * PIECE
PIECE_COLS = PIECE // 16

CLOCK_BAR_COLUMNS = 1024
WARMERS = CLOCK_BAR_COLUMNS // P

FLOPS = 2 * P * P * ENTRIES

BF16 = mybir.dt.bfloat16
F32 = mybir.dt.float32
U16 = mybir.dt.uint16


def tile_scatter_matmul_kernel(tc, base, x, w, b, offs, out):
    nc = tc.nc
    identity_function = mybir.ActivationFunctionType.Identity
    with (
        tc.tile_pool(name="held", bufs=1) as held,
        tc.psum_pool(name="windows", bufs=1) as windows,
    ):
        both_bases = held.tile([P, SEQS, TOKENS], BF16, name="both_bases")
        nc.sync.dma_start(both_bases[:], base.rearrange("i m t -> m i t"))
        weights = held.tile([P, P], BF16, name="weights")
        nc.sync.dma_start(weights[:], w)
        moving = held.tile([P, ENTRIES], BF16, name="moving")
        nc.sync.dma_start(moving[:], x)
        offsets = held.tile([P, ENTRIES // 16], U16, name="offsets")
        nc.sync.dma_start(offsets[:], offs)
        bias = held.tile([P, 1], F32, name="bias")
        nc.sync.dma_start(bias[:], b)

        zeros = held.tile([P, P], BF16, name="zeros")
        nc.vector.memset(zeros[:], 0.0)
        unread = windows.tile([P, P], F32, name="unread")
        for warmer in range(WARMERS):
            nc.tensor.matmul(unread[:], zeros[:], zeros[:], start=True, stop=True)

        identity = held.tile([P, P], BF16, name="identity")
        make_identity(nc, identity[:])

        table_warmer = held.tile([P, 1], F32, name="table_warmer")
        nc.vector.memset(table_warmer[:], 0.0)
        nc.scalar.activation(table_warmer[:], table_warmer[:], identity_function)

        window_tiles = [windows.tile([P, TOKENS], F32, name=f"window{i}") for i in range(SEQS)]
        for i in range(SEQS):
            nc.tensor.matmul(window_tiles[i][:], identity[:], both_bases[:, i, :], start=True, stop=False)

        for i in range(SEQS):
            nc.tensor.matmul(
                window_tiles[i][:].indirect(offsets[:, i * PIECE_COLS : (i + 1) * PIECE_COLS]),
                weights[:],
                moving[:, i * PIECE : (i + 1) * PIECE],
                start=False,
                stop=True,
            )

        result_tiles = [held.tile([P, TOKENS], F32, name=f"result{i}") for i in range(SEQS)]
        nc.scalar.activation(result_tiles[0][:], window_tiles[0][:], identity_function, bias=bias[:, 0:1])
        nc.scalar.dma_start(out[0], result_tiles[0][:])
        nc.vector.tensor_scalar_add(result_tiles[1][:], window_tiles[1][:], bias[:, 0:1])
        nc.scalar.dma_start(out[1], result_tiles[1][:])
